import numpy as np
import ml_dtypes


def mxq(x, axis, fmt="e4m3"):
    dtype, down = {"e4m3": (ml_dtypes.float8_e4m3fn, 7), "e5m2": (ml_dtypes.float8_e5m2, 14)}[fmt]
    v = np.moveaxis(np.asarray(x, np.float32).astype(ml_dtypes.bfloat16).astype(np.float64), axis, -1)
    blocks = v.reshape(v.shape[:-1] + (-1, 32))
    amax = np.abs(blocks).max(-1, keepdims=True)
    byte = np.maximum(np.where(amax > 0, np.frexp(amax)[1] - 1 + 127, 0) - down, 1)
    scale = np.exp2(byte - 127.0)
    codes = (blocks / scale).astype(np.float32).astype(dtype).astype(np.float64)
    return np.moveaxis((codes * scale).reshape(v.shape), -1, axis)


WIDE = False


def mx_kscale(k):
    if not WIDE:
        return np.ones(k)
    levels = np.array([10, -10, 5, -5, 0])
    if k % 512:
        return np.exp2(np.random.permutation(np.resize(levels, k // 32))).repeat(32)
    a = np.empty((k // 512, 16))
    for p in range(k // 512):
        a[p, :8] = np.random.permutation(np.resize(levels, 8))
        for g in range(8):
            far = levels[np.abs(levels - a[p, g]) >= 10]
            a[p, g + 8] = far[np.random.randint(len(far))]
    return np.exp2(a.ravel()).repeat(32)


def f64(x):
    return np.asarray(x).astype(np.float64)


def striped(idx):
    return np.tile(np.asarray(idx).reshape(-1, 16).T, (8, 1)).astype(np.uint16)


def unstriped(offs):
    return offs[:16].T.reshape(-1).astype(np.int64)


E2M1 = np.array([0.0, 0.5, 1.0, 1.5, 2.0, 3.0, 4.0, 6.0, -0.0, -0.5, -1.0, -1.5, -2.0, -3.0, -4.0, -6.0])


def pack_weight(w, fmt):
    k, n = w.shape
    w = f64(np.asarray(w, np.float32).astype(ml_dtypes.bfloat16)).reshape(k // 32, 32, n)
    amax = np.abs(w).max(1)
    if fmt == "e4m3":
        byte = np.frexp(amax)[1] - 1 + 127 - 7
    else:
        mant, ex = np.frexp(amax / 6.0)
        byte = np.where(mant > 0.5, ex, ex - 1) + 127
    byte = np.clip(np.where(amax > 0, byte, 1), 1, 254)
    scaled = (w * np.exp2(127.0 - byte)[:, None, :]).reshape(k, n).astype(np.float32)
    by_word = np.ascontiguousarray(scaled.reshape(k // 512, 128, 4, n).transpose(0, 1, 3, 2))
    if fmt == "e4m3":
        words = by_word.astype(ml_dtypes.float8_e4m3fn).view(np.uint8)
    else:
        c = by_word.astype(ml_dtypes.float4_e2m1fn).view(np.uint8) & 0xF
        words = (c[..., 0::2] | (c[..., 1::2] << 4)).reshape(k // 512, 128, 2 * n)
    return np.ascontiguousarray(words), np.ascontiguousarray(byte.astype(np.uint8).reshape(k // 512, 16, n))


def unpack_weight(words, scales, fmt):
    g, _, n = scales.shape
    words = np.ascontiguousarray(words).reshape(g, 128, n, -1)
    if fmt == "e4m3":
        vals = words.view(ml_dtypes.float8_e4m3fn).astype(np.float64)
    else:
        nib = np.empty((g, 128, n, 4), np.uint8)
        nib[..., 0::2] = words & 0xF
        nib[..., 1::2] = words >> 4
        vals = E2M1[nib]
    vals = vals * np.repeat(np.exp2(scales.astype(np.float64) - 127.0), 8, axis=1)[..., None]
    return vals.transpose(0, 1, 3, 2).reshape(g * 512, n)


D, T, V, I, Q = 512, 4096, 2048, 512, 128


def setup_inputs():
    n = np.random.standard_normal
    idx = np.random.permutation(T)[:V]
    idx2 = np.random.permutation(V)[:I]
    fd = mx_kscale(D)
    vocp = pack_weight(n((D, T)) / fd[:, None], "e2m1")
    return {
        "hid": (n((D, Q)) * 1.0 / np.sqrt(D) * fd[:, None]).astype(np.float32),
        "voc_words": vocp[0],
        "voc_scales": vocp[1],
        "fore": (np.random.uniform(0.1, 1.0, (Q, I))).astype(np.float32),
        "back": (np.random.uniform(0.1, 1.0, (Q, I))).astype(np.float32),
        "offs": striped(idx),
        "offs2": striped(idx2),
    }


def reference(hid, voc_words, voc_scales, fore, back, offs, offs2):
    idx = unstriped(offs)
    idx2 = unstriped(offs2)
    vocu = unpack_weight(voc_words, voc_scales, "e2m1")
    hidq = mxq(f64(hid), 0, "e4m3")
    vocidxg = vocu[:, idx]
    a = hidq.T @ vocidxg
    p = np.exp(a - np.max(a, axis=1, keepdims=True))
    g = f64(fore) * f64(back)
    gn = g / np.sum(g, axis=1, keepdims=True)
    gf = np.zeros((Q, V))
    gf[:, idx2] = gn
    y = (p / np.sum(p, axis=1, keepdims=True) - gf) * 2048.0
    return y

@@ -1,0 +1,146 @@
+from contextlib import ExitStack
+
+import concourse.mybir as mybir
+
+F32 = mybir.dt.float32
+BF16 = mybir.dt.bfloat16
+I32 = mybir.dt.int32
+U32 = mybir.dt.uint32
+U16 = mybir.dt.uint16
+U8 = mybir.dt.uint8
+FP8X4 = mybir.dt.float8_e4m3fn_x4
+FP4X4 = mybir.dt.float4_e2m1fn_x4
+ALU = mybir.AluOpType
+ACT = mybir.ActivationFunctionType
+
+P = 128
+PACK = 4
+D, T, V, I, Q = 512, 4096, 2048, 512, 128
+BANK = 512
+LIST_GROUP = 16
+WORD_PIECE = 1024
+OUT_SCALE = 2048.0
+
+FLOPS = 2 * D * V * Q
+
+
+def tile_attend_glabels_kernel(tc, hid, voc_words, voc_scales, fore, back, offs, offs2, out):
+    nc = tc.nc
+    banks = V // BANK
+
+    with ExitStack() as ctx:
+        keep = ctx.enter_context(tc.tile_pool(name="keep", bufs=1))
+        psum = ctx.enter_context(tc.psum_pool(name="psum", bufs=1))
+
+        entry_list = keep.tile([P, V // LIST_GROUP], U16, name="entry_list")
+        label_list = keep.tile([P, I // LIST_GROUP], U16, name="label_list")
+        store_words = keep.tile([P, T], U16, name="store_words", align_bytes=64)
+        store_scales = keep.tile([P, T], U8, name="store_scales", align_bytes=64)
+        hid_raw = keep.tile([P, PACK, Q], F32, name="hid_raw")
+        fore_sb = keep.tile([P, I], F32, name="fore_sb")
+        back_sb = keep.tile([P, I], F32, name="back_sb")
+        labels = keep.tile([P, V], F32, name="labels")
+
+        warm_in = keep.tile([P, 1], F32, name="warm_in")
+        warm_out = keep.tile([P, 1], F32, name="warm_out")
+        nc.gpsimd.memset(warm_in[:], 0.0)
+        nc.scalar.activation(out=warm_out[:], in_=warm_in[:], func=ACT.Exp)
+
+        nc.vector.memset(store_scales[:].bitcast(I32), 0)
+        nc.vector.memset(labels[:], 0.0)
+
+        nc.sync.dma_start(entry_list[:], offs)
+        nc.sync.dma_start(store_words[:].bitcast(I32), voc_words[0].bitcast(I32))
+        for quad in range(4):
+            nc.sync.dma_start(
+                store_scales[32 * quad : 32 * quad + 4, :].bitcast(I32),
+                voc_scales[0, 4 * quad : 4 * quad + 4, :].bitcast(I32),
+            )
+        nc.sync.dma_start(hid_raw[:], hid.rearrange("(p j) q -> p j q", j=PACK))
+        nc.sync.dma_start(fore_sb[:], fore)
+        nc.sync.dma_start(back_sb[:], back)
+        nc.sync.dma_start(label_list[:], offs2)
+
+        words = []
+        for lo in range(0, V, WORD_PIECE):
+            piece = keep.tile([P, WORD_PIECE], U16, name="words%d" % lo, align_bytes=64)
+            words.extend(piece[:, c : c + BANK] for c in range(0, WORD_PIECE, BANK))
+            nc.vector.tensor_copy(
+                piece[:],
+                store_words[:].indirect(entry_list[:, lo // LIST_GROUP : (lo + WORD_PIECE) // LIST_GROUP]),
+            )
+
+        hid_bf = keep.tile([P, Q, PACK], BF16, name="hid_bf", align_bytes=64)
+        nc.scalar.copy(out=hid_bf[:], in_=hid_raw[:].rearrange("p j q -> p q j"))
+        hid_codes = keep.tile([P, Q], U32, name="hid_codes", align_bytes=64)
+        hid_scales = keep.tile([P, Q], U8, name="hid_scales", align_bytes=64)
+        nc.vector.quantize_mx(
+            out=hid_codes[:].bitcast(FP8X4),
+            scales=hid_scales[:],
+            in_=hid_bf[:].rearrange("p q j -> p (q j)"),
+        )
+
+        prod = keep.tile([P, I], F32, name="prod")
+        prod_sum = keep.tile([P, 1], F32, name="prod_sum")
+        fore_n = keep.tile([P, I], F32, name="fore_n")
+        nc.vector.scalar_tensor_tensor(
+            out=prod[:], in0=fore_sb[:], scalar=1.0 / OUT_SCALE, in1=back_sb[:],
+            op0=ALU.mult, op1=ALU.mult, accum_out=prod_sum[:],
+        )
+
+        scales = [keep.tile([P, BANK], U8, name="scales%d" % b, align_bytes=64) for b in range(banks)]
+        neg = keep.tile([P, V], F32, name="neg")
+        neg_max = [keep.tile([P, 1], F32, name="neg_max%d" % b) for b in range(banks)]
+        scores = [psum.tile([P, BANK], F32, name="scores%d" % b) for b in range(banks)]
+
+        def gather_and_score(b):
+            nc.vector.tensor_copy(
+                scales[b][:],
+                store_scales[:].indirect(entry_list[:, b * BANK // LIST_GROUP : (b + 1) * BANK // LIST_GROUP]),
+            )
+            nc.tensor.matmul_mx(
+                out=scores[b][:],
+                lhsT=hid_codes[:].bitcast(FP8X4),
+                lhsT_scale=hid_scales[:],
+                rhs=words[b].bitcast(FP4X4),
+                rhs_scale=scales[b][:],
+                start=True,
+                stop=True,
+            )
+
+        def running_max(b):
+            nc.vector.tensor_scalar(
+                out=neg[:, b * BANK : (b + 1) * BANK], in0=scores[b][:],
+                scalar1=-1.0, scalar2=neg_max[b - 1][:] if b else None,
+                op0=ALU.mult, op1=ALU.min, accum_out=neg_max[b][:],
+            )
+
+        gather_and_score(0)
+        for b in range(1, banks):
+            gather_and_score(b)
+            running_max(b - 1)
+        prod_inv = neg_max[banks - 3]
+        nc.vector.reciprocal(prod_inv[:], prod_sum[:])
+        nc.scalar.activation(out=fore_n[:], in_=fore_sb[:], func=ACT.Copy, scale=prod_inv[:])
+        running_max(banks - 1)
+
+        expd = keep.tile([P, V], F32, name="expd")
+        exp_sum = keep.tile([P, 1], F32, name="exp_sum")
+        exp_sum_s = keep.tile([P, 1], F32, name="exp_sum_s")
+        exp_inv = keep.tile([P, 1], F32, name="exp_inv")
+        nc.scalar.activation(
+            out=expd[:], in_=neg[:], func=ACT.Exp, scale=-1.0, bias=neg_max[banks - 1][:], accum_out=exp_sum[:]
+        )
+        nc.scalar.activation(out=exp_sum_s[:], in_=exp_sum[:], func=ACT.Copy, scale=1.0 / OUT_SCALE)
+
+        nc.vector.tensor_tensor(labels[:].indirect(label_list[:]), fore_n[:], back_sb[:], ALU.mult)
+        nc.vector.reciprocal(exp_inv[:], exp_sum_s[:])
+
+        for b in range(banks):
+            cols = slice(b * BANK, (b + 1) * BANK)
+            result = keep.tile([P, BANK], F32, name="result%d" % b)
+            nc.vector.scalar_tensor_tensor(
+                out=result[:], in0=expd[:, cols], scalar=exp_inv[:], in1=labels[:, cols],
+                op0=ALU.mult, op1=ALU.subtract,
+            )
+            nc.sync.dma_start(out[:, cols], result[:])

@@ -18,7 +18,8 @@ PACK = 4
 D, T, V, I, Q = 512, 4096, 2048, 512, 128
 BANK = 512
 LIST_GROUP = 16
-WORD_PIECE = 1024
+STORE = 256
+SCALE_PIECE = 1024
 OUT_SCALE = 2048.0
 
 FLOPS = 2 * D * V * Q
@@ -30,49 +31,49 @@ def tile_attend_glabels_kernel(tc, hid, voc_words, voc_scales, fore, back, offs,
 
     with ExitStack() as ctx:
         keep = ctx.enter_context(tc.tile_pool(name="keep", bufs=1))
+        ring = ctx.enter_context(tc.tile_pool(name="ring", bufs=1))
         psum = ctx.enter_context(tc.psum_pool(name="psum", bufs=1))
 
         entry_list = keep.tile([P, V // LIST_GROUP], U16, name="entry_list")
         label_list = keep.tile([P, I // LIST_GROUP], U16, name="label_list")
         store_words = keep.tile([P, T], U16, name="store_words", align_bytes=64)
-        store_scales = keep.tile([P, T], U8, name="store_scales", align_bytes=64)
+        store_scales = keep.tile([P, T], U8, name="store_scales", tag="store_scales_then_hid_codes", align_bytes=64)
         hid_raw = keep.tile([P, PACK, Q], F32, name="hid_raw")
         fore_sb = keep.tile([P, I], F32, name="fore_sb")
         back_sb = keep.tile([P, I], F32, name="back_sb")
         labels = keep.tile([P, V], F32, name="labels")
 
-        warm_in = keep.tile([P, 1], F32, name="warm_in")
-        warm_out = keep.tile([P, 1], F32, name="warm_out")
-        nc.gpsimd.memset(warm_in[:], 0.0)
-        nc.scalar.activation(out=warm_out[:], in_=warm_in[:], func=ACT.Exp)
-
+        planes = [
+            keep.tile([P, SCALE_PIECE], U8, name="plane%d" % h, align_bytes=64) for h in range(V // SCALE_PIECE)
+        ]
         nc.vector.memset(store_scales[:].bitcast(I32), 0)
+        for plane in planes:
+            nc.vector.memset(plane[:].bitcast(I32), 0)
         nc.vector.memset(labels[:], 0.0)
 
         nc.sync.dma_start(entry_list[:], offs)
-        nc.sync.dma_start(store_words[:].bitcast(I32), voc_words[0].bitcast(I32))
-        for quad in range(4):
-            nc.sync.dma_start(
-                store_scales[32 * quad : 32 * quad + 4, :].bitcast(I32),
-                voc_scales[0, 4 * quad : 4 * quad + 4, :].bitcast(I32),
-            )
         nc.sync.dma_start(hid_raw[:], hid.rearrange("(p j) q -> p j q", j=PACK))
+        nc.sync.dma_start(store_scales[0:P:8, :].bitcast(I32), voc_scales[0].bitcast(I32))
+        nc.sync.dma_start(label_list[:], offs2)
         nc.sync.dma_start(fore_sb[:], fore)
         nc.sync.dma_start(back_sb[:], back)
-        nc.sync.dma_start(label_list[:], offs2)
+        nc.sync.dma_start(store_words[:].bitcast(I32), voc_words[0].bitcast(I32))
 
-        words = []
-        for lo in range(0, V, WORD_PIECE):
-            piece = keep.tile([P, WORD_PIECE], U16, name="words%d" % lo, align_bytes=64)
-            words.extend(piece[:, c : c + BANK] for c in range(0, WORD_PIECE, BANK))
+        for lo in range(0, V, SCALE_PIECE):
+            spread = keep.tile([P, SCALE_PIECE], U8, name="spread%d" % lo, align_bytes=64)
             nc.vector.tensor_copy(
-                piece[:],
-                store_words[:].indirect(entry_list[:, lo // LIST_GROUP : (lo + WORD_PIECE) // LIST_GROUP]),
+                spread[:],
+                store_scales[:].indirect(entry_list[:, lo // LIST_GROUP : (lo + SCALE_PIECE) // LIST_GROUP]),
             )
+            for quad in range(4):
+                nc.sync.dma_start(
+                    planes[lo // SCALE_PIECE][32 * quad : 32 * quad + 4, :].bitcast(I32),
+                    spread[32 * quad : 32 * quad + 32 : 8, :].bitcast(I32),
+                )
 
-        hid_bf = keep.tile([P, Q, PACK], BF16, name="hid_bf", align_bytes=64)
+        hid_bf = ring.tile([P, Q, PACK], BF16, name="hid_bf", align_bytes=64, offset=BANK)
         nc.scalar.copy(out=hid_bf[:], in_=hid_raw[:].rearrange("p j q -> p q j"))
-        hid_codes = keep.tile([P, Q], U32, name="hid_codes", align_bytes=64)
+        hid_codes = keep.tile([P, Q], U32, name="hid_codes", tag="store_scales_then_hid_codes", align_bytes=64)
         hid_scales = keep.tile([P, Q], U8, name="hid_scales", align_bytes=64)
         nc.vector.quantize_mx(
             out=hid_codes[:].bitcast(FP8X4),
@@ -82,28 +83,29 @@ def tile_attend_glabels_kernel(tc, hid, voc_words, voc_scales, fore, back, offs,
 
         prod = keep.tile([P, I], F32, name="prod")
         prod_sum = keep.tile([P, 1], F32, name="prod_sum")
-        fore_n = keep.tile([P, I], F32, name="fore_n")
+        prod_inv = keep.tile([P, 1], F32, name="prod_inv")
         nc.vector.scalar_tensor_tensor(
             out=prod[:], in0=fore_sb[:], scalar=1.0 / OUT_SCALE, in1=back_sb[:],
             op0=ALU.mult, op1=ALU.mult, accum_out=prod_sum[:],
         )
+        nc.vector.reciprocal(prod_inv[:], prod_sum[:])
 
-        scales = [keep.tile([P, BANK], U8, name="scales%d" % b, align_bytes=64) for b in range(banks)]
         neg = keep.tile([P, V], F32, name="neg")
         neg_max = [keep.tile([P, 1], F32, name="neg_max%d" % b) for b in range(banks)]
         scores = [psum.tile([P, BANK], F32, name="scores%d" % b) for b in range(banks)]
 
         def gather_and_score(b):
+            words = ring.tile([P, BANK], U16, name="words%d" % b, align_bytes=64, offset=2 * BANK * (b % 2))
             nc.vector.tensor_copy(
-                scales[b][:],
-                store_scales[:].indirect(entry_list[:, b * BANK // LIST_GROUP : (b + 1) * BANK // LIST_GROUP]),
+                words[:],
+                store_words[:].indirect(entry_list[:, b * BANK // LIST_GROUP : (b + 1) * BANK // LIST_GROUP]),
             )
             nc.tensor.matmul_mx(
                 out=scores[b][:],
                 lhsT=hid_codes[:].bitcast(FP8X4),
                 lhsT_scale=hid_scales[:],
-                rhs=words[b].bitcast(FP4X4),
-                rhs_scale=scales[b][:],
+                rhs=words[:].bitcast(FP4X4),
+                rhs_scale=planes[b * BANK // SCALE_PIECE][:, b * BANK % SCALE_PIECE : b * BANK % SCALE_PIECE + BANK],
                 start=True,
                 stop=True,
             )
@@ -119,8 +121,7 @@ def tile_attend_glabels_kernel(tc, hid, voc_words, voc_scales, fore, back, offs,
         for b in range(1, banks):
             gather_and_score(b)
             running_max(b - 1)
-        prod_inv = neg_max[banks - 3]
-        nc.vector.reciprocal(prod_inv[:], prod_sum[:])
+        fore_n = ring.tile([P, I], F32, name="fore_n", align_bytes=64, offset=2 * BANK)
         nc.scalar.activation(out=fore_n[:], in_=fore_sb[:], func=ACT.Copy, scale=prod_inv[:])
         running_max(banks - 1)
 
@@ -136,9 +137,9 @@ def tile_attend_glabels_kernel(tc, hid, voc_words, voc_scales, fore, back, offs,
         nc.vector.tensor_tensor(labels[:].indirect(label_list[:]), fore_n[:], back_sb[:], ALU.mult)
         nc.vector.reciprocal(exp_inv[:], exp_sum_s[:])
 
-        for b in range(banks):
-            cols = slice(b * BANK, (b + 1) * BANK)
-            result = keep.tile([P, BANK], F32, name="result%d" % b)
+        for b in range(V // STORE):
+            cols = slice(b * STORE, (b + 1) * STORE)
+            result = keep.tile([P, STORE], F32, name="result%d" % b)
             nc.vector.scalar_tensor_tensor(
                 out=result[:], in0=expd[:, cols], scalar=exp_inv[:], in1=labels[:, cols],
                 op0=ALU.mult, op1=ALU.subtract,

@@ -37,7 +37,7 @@ def tile_attend_glabels_kernel(tc, hid, voc_words, voc_scales, fore, back, offs,
         entry_list = keep.tile([P, V // LIST_GROUP], U16, name="entry_list")
         label_list = keep.tile([P, I // LIST_GROUP], U16, name="label_list")
         store_words = keep.tile([P, T], U16, name="store_words", align_bytes=64)
-        store_scales = keep.tile([P, T], U8, name="store_scales", tag="store_scales_then_hid_codes", align_bytes=64)
+        store_scales = keep.tile([P, T], U8, name="store_scales", align_bytes=64)
         hid_raw = keep.tile([P, PACK, Q], F32, name="hid_raw")
         fore_sb = keep.tile([P, I], F32, name="fore_sb")
         back_sb = keep.tile([P, I], F32, name="back_sb")
@@ -51,13 +51,22 @@ def tile_attend_glabels_kernel(tc, hid, voc_words, voc_scales, fore, back, offs,
             nc.vector.memset(plane[:].bitcast(I32), 0)
         nc.vector.memset(labels[:], 0.0)
 
-        nc.sync.dma_start(entry_list[:], offs)
-        nc.sync.dma_start(hid_raw[:], hid.rearrange("(p j) q -> p j q", j=PACK))
-        nc.sync.dma_start(store_scales[0:P:8, :].bitcast(I32), voc_scales[0].bitcast(I32))
-        nc.sync.dma_start(label_list[:], offs2)
         nc.sync.dma_start(fore_sb[:], fore)
         nc.sync.dma_start(back_sb[:], back)
+        nc.sync.dma_start(entry_list[:], offs)
+        nc.sync.dma_start(store_scales[0:P:8, :].bitcast(I32), voc_scales[0].bitcast(I32))
+        nc.sync.dma_start(hid_raw[:], hid.rearrange("(p j) q -> p j q", j=PACK))
+        nc.sync.dma_start(label_list[:], offs2)
         nc.sync.dma_start(store_words[:].bitcast(I32), voc_words[0].bitcast(I32))
+
+        prod = keep.tile([P, I], F32, name="prod")
+        prod_sum = keep.tile([P, 1], F32, name="prod_sum")
+        prod_inv = keep.tile([P, 1], F32, name="prod_inv")
+        prod_small = keep.tile([P, I], F32, name="prod_small")
+        nc.vector.tensor_tensor(prod[:], fore_sb[:], back_sb[:], ALU.mult)
+        nc.scalar.activation(
+            out=prod_small[:], in_=prod[:], func=ACT.Copy, scale=1.0 / OUT_SCALE, accum_out=prod_sum[:]
+        )
 
         for lo in range(0, V, SCALE_PIECE):
             spread = keep.tile([P, SCALE_PIECE], U8, name="spread%d" % lo, align_bytes=64)
@@ -71,9 +80,9 @@ def tile_attend_glabels_kernel(tc, hid, voc_words, voc_scales, fore, back, offs,
                     spread[32 * quad : 32 * quad + 32 : 8, :].bitcast(I32),
                 )
 
-        hid_bf = ring.tile([P, Q, PACK], BF16, name="hid_bf", align_bytes=64, offset=BANK)
+        hid_bf = keep.tile([P, Q, PACK], BF16, name="hid_bf", align_bytes=64)
         nc.scalar.copy(out=hid_bf[:], in_=hid_raw[:].rearrange("p j q -> p q j"))
-        hid_codes = keep.tile([P, Q], U32, name="hid_codes", tag="store_scales_then_hid_codes", align_bytes=64)
+        hid_codes = keep.tile([P, Q], U32, name="hid_codes", align_bytes=64)
         hid_scales = keep.tile([P, Q], U8, name="hid_scales", align_bytes=64)
         nc.vector.quantize_mx(
             out=hid_codes[:].bitcast(FP8X4),
@@ -81,13 +90,6 @@ def tile_attend_glabels_kernel(tc, hid, voc_words, voc_scales, fore, back, offs,
             in_=hid_bf[:].rearrange("p q j -> p (q j)"),
         )
 
-        prod = keep.tile([P, I], F32, name="prod")
-        prod_sum = keep.tile([P, 1], F32, name="prod_sum")
-        prod_inv = keep.tile([P, 1], F32, name="prod_inv")
-        nc.vector.scalar_tensor_tensor(
-            out=prod[:], in0=fore_sb[:], scalar=1.0 / OUT_SCALE, in1=back_sb[:],
-            op0=ALU.mult, op1=ALU.mult, accum_out=prod_sum[:],
-        )
         nc.vector.reciprocal(prod_inv[:], prod_sum[:])
 
         neg = keep.tile([P, V], F32, name="neg")
@@ -122,7 +124,7 @@ def tile_attend_glabels_kernel(tc, hid, voc_words, voc_scales, fore, back, offs,
             gather_and_score(b)
             running_max(b - 1)
         fore_n = ring.tile([P, I], F32, name="fore_n", align_bytes=64, offset=2 * BANK)
-        nc.scalar.activation(out=fore_n[:], in_=fore_sb[:], func=ACT.Copy, scale=prod_inv[:])
+        nc.scalar.activation(out=fore_n[:], in_=prod[:], func=ACT.Copy, scale=prod_inv[:])
         running_max(banks - 1)
 
         expd = keep.tile([P, V], F32, name="expd")
@@ -134,7 +136,7 @@ def tile_attend_glabels_kernel(tc, hid, voc_words, voc_scales, fore, back, offs,
         )
         nc.scalar.activation(out=exp_sum_s[:], in_=exp_sum[:], func=ACT.Copy, scale=1.0 / OUT_SCALE)
 
-        nc.vector.tensor_tensor(labels[:].indirect(label_list[:]), fore_n[:], back_sb[:], ALU.mult)
+        nc.vector.tensor_copy(labels[:].indirect(label_list[:]), fore_n[:])
         nc.vector.reciprocal(exp_inv[:], exp_sum_s[:])
 
         for b in range(V // STORE):

from contextlib import ExitStack

import concourse.mybir as mybir

F32 = mybir.dt.float32
BF16 = mybir.dt.bfloat16
I32 = mybir.dt.int32
U32 = mybir.dt.uint32
U16 = mybir.dt.uint16
U8 = mybir.dt.uint8
FP8X4 = mybir.dt.float8_e4m3fn_x4
FP4X4 = mybir.dt.float4_e2m1fn_x4
ALU = mybir.AluOpType
ACT = mybir.ActivationFunctionType

P = 128
PACK = 4
D, T, V, I, Q = 512, 4096, 2048, 512, 128
BANK = 512
LIST_GROUP = 16
STORE = 256
SCALE_PIECE = 1024
OUT_SCALE = 2048.0

FLOPS = 2 * D * V * Q


def tile_attend_glabels_kernel(tc, hid, voc_words, voc_scales, fore, back, offs, offs2, out):
    nc = tc.nc
    banks = V // BANK

    with ExitStack() as ctx:
        keep = ctx.enter_context(tc.tile_pool(name="keep", bufs=1))
        ring = ctx.enter_context(tc.tile_pool(name="ring", bufs=1))
        psum = ctx.enter_context(tc.psum_pool(name="psum", bufs=1))

        entry_list = keep.tile([P, V // LIST_GROUP], U16, name="entry_list")
        label_list = keep.tile([P, I // LIST_GROUP], U16, name="label_list")
        store_words = keep.tile([P, T], U16, name="store_words", align_bytes=64)
        store_scales = keep.tile([P, T], U8, name="store_scales", align_bytes=64)
        hid_raw = keep.tile([P, PACK, Q], F32, name="hid_raw")
        fore_sb = keep.tile([P, I], F32, name="fore_sb")
        back_sb = keep.tile([P, I], F32, name="back_sb")
        labels = keep.tile([P, V], F32, name="labels")

        planes = [
            keep.tile([P, SCALE_PIECE], U8, name="plane%d" % h, align_bytes=64) for h in range(V // SCALE_PIECE)
        ]
        nc.vector.memset(store_scales[:].bitcast(I32), 0)
        for plane in planes:
            nc.vector.memset(plane[:].bitcast(I32), 0)
        nc.vector.memset(labels[:], 0.0)

        nc.sync.dma_start(fore_sb[:], fore)
        nc.sync.dma_start(back_sb[:], back)
        nc.sync.dma_start(entry_list[:], offs)
        nc.sync.dma_start(store_scales[0:P:8, :].bitcast(I32), voc_scales[0].bitcast(I32))
        nc.sync.dma_start(hid_raw[:], hid.rearrange("(p j) q -> p j q", j=PACK))
        nc.sync.dma_start(label_list[:], offs2)
        nc.sync.dma_start(store_words[:].bitcast(I32), voc_words[0].bitcast(I32))

        prod = keep.tile([P, I], F32, name="prod")
        prod_sum = keep.tile([P, 1], F32, name="prod_sum")
        prod_inv = keep.tile([P, 1], F32, name="prod_inv")
        prod_small = keep.tile([P, I], F32, name="prod_small")
        nc.vector.tensor_tensor(prod[:], fore_sb[:], back_sb[:], ALU.mult)
        nc.scalar.activation(
            out=prod_small[:], in_=prod[:], func=ACT.Copy, scale=1.0 / OUT_SCALE, accum_out=prod_sum[:]
        )

        for lo in range(0, V, SCALE_PIECE):
            spread = keep.tile([P, SCALE_PIECE], U8, name="spread%d" % lo, align_bytes=64)
            nc.vector.tensor_copy(
                spread[:],
                store_scales[:].indirect(entry_list[:, lo // LIST_GROUP : (lo + SCALE_PIECE) // LIST_GROUP]),
            )
            for quad in range(4):
                nc.sync.dma_start(
                    planes[lo // SCALE_PIECE][32 * quad : 32 * quad + 4, :].bitcast(I32),
                    spread[32 * quad : 32 * quad + 32 : 8, :].bitcast(I32),
                )

        hid_bf = keep.tile([P, Q, PACK], BF16, name="hid_bf", align_bytes=64)
        nc.scalar.copy(out=hid_bf[:], in_=hid_raw[:].rearrange("p j q -> p q j"))
        hid_codes = keep.tile([P, Q], U32, name="hid_codes", align_bytes=64)
        hid_scales = keep.tile([P, Q], U8, name="hid_scales", align_bytes=64)
        nc.vector.quantize_mx(
            out=hid_codes[:].bitcast(FP8X4),
            scales=hid_scales[:],
            in_=hid_bf[:].rearrange("p q j -> p (q j)"),
        )

        nc.vector.reciprocal(prod_inv[:], prod_sum[:])

        neg = keep.tile([P, V], F32, name="neg")
        neg_max = [keep.tile([P, 1], F32, name="neg_max%d" % b) for b in range(banks)]
        scores = [psum.tile([P, BANK], F32, name="scores%d" % b) for b in range(banks)]

        def gather_and_score(b):
            words = ring.tile([P, BANK], U16, name="words%d" % b, align_bytes=64, offset=2 * BANK * (b % 2))
            nc.vector.tensor_copy(
                words[:],
                store_words[:].indirect(entry_list[:, b * BANK // LIST_GROUP : (b + 1) * BANK // LIST_GROUP]),
            )
            nc.tensor.matmul_mx(
                out=scores[b][:],
                lhsT=hid_codes[:].bitcast(FP8X4),
                lhsT_scale=hid_scales[:],
                rhs=words[:].bitcast(FP4X4),
                rhs_scale=planes[b * BANK // SCALE_PIECE][:, b * BANK % SCALE_PIECE : b * BANK % SCALE_PIECE + BANK],
                start=True,
                stop=True,
            )

        def running_max(b):
            nc.vector.tensor_scalar(
                out=neg[:, b * BANK : (b + 1) * BANK], in0=scores[b][:],
                scalar1=-1.0, scalar2=neg_max[b - 1][:] if b else None,
                op0=ALU.mult, op1=ALU.min, accum_out=neg_max[b][:],
            )

        gather_and_score(0)
        for b in range(1, banks):
            gather_and_score(b)
            running_max(b - 1)
        fore_n = ring.tile([P, I], F32, name="fore_n", align_bytes=64, offset=2 * BANK)
        nc.scalar.activation(out=fore_n[:], in_=prod[:], func=ACT.Copy, scale=prod_inv[:])
        running_max(banks - 1)

        expd = keep.tile([P, V], F32, name="expd")
        exp_sum = keep.tile([P, 1], F32, name="exp_sum")
        exp_sum_s = keep.tile([P, 1], F32, name="exp_sum_s")
        exp_inv = keep.tile([P, 1], F32, name="exp_inv")
        nc.scalar.activation(
            out=expd[:], in_=neg[:], func=ACT.Exp, scale=-1.0, bias=neg_max[banks - 1][:], accum_out=exp_sum[:]
        )
        nc.scalar.activation(out=exp_sum_s[:], in_=exp_sum[:], func=ACT.Copy, scale=1.0 / OUT_SCALE)

        nc.vector.tensor_copy(labels[:].indirect(label_list[:]), fore_n[:])
        nc.vector.reciprocal(exp_inv[:], exp_sum_s[:])

        for b in range(V // STORE):
            cols = slice(b * STORE, (b + 1) * STORE)
            result = keep.tile([P, STORE], F32, name="result%d" % b)
            nc.vector.scalar_tensor_tensor(
                out=result[:], in0=expd[:, cols], scalar=exp_inv[:], in1=labels[:, cols],
                op0=ALU.mult, op1=ALU.subtract,
            )
            nc.sync.dma_start(out[:, cols], result[:])
